import numpy as np
import ml_dtypes


def mxq(x, axis, fmt="e4m3"):
    dtype, down = {"e4m3": (ml_dtypes.float8_e4m3fn, 7), "e5m2": (ml_dtypes.float8_e5m2, 14)}[fmt]
    v = np.moveaxis(np.asarray(x, np.float32).astype(ml_dtypes.bfloat16).astype(np.float64), axis, -1)
    blocks = v.reshape(v.shape[:-1] + (-1, 32))
    amax = np.abs(blocks).max(-1, keepdims=True)
    byte = np.maximum(np.where(amax > 0, np.frexp(amax)[1] - 1 + 127, 0) - down, 1)
    scale = np.exp2(byte - 127.0)
    codes = (blocks / scale).astype(np.float32).astype(dtype).astype(np.float64)
    return np.moveaxis((codes * scale).reshape(v.shape), -1, axis)


WIDE = False


def mx_kscale(k):
    if not WIDE:
        return np.ones(k)
    levels = np.array([10, -10, 5, -5, 0])
    if k % 512:
        return np.exp2(np.random.permutation(np.resize(levels, k // 32))).repeat(32)
    a = np.empty((k // 512, 16))
    for p in range(k // 512):
        a[p, :8] = np.random.permutation(np.resize(levels, 8))
        for g in range(8):
            far = levels[np.abs(levels - a[p, g]) >= 10]
            a[p, g + 8] = far[np.random.randint(len(far))]
    return np.exp2(a.ravel()).repeat(32)


def f64(x):
    return np.asarray(x).astype(np.float64)


def striped(idx):
    return np.tile(idx.reshape(-1, 16).T, (8, 1)).astype(np.uint16)


def unstriped(offs):
    return offs[:16].T.reshape(-1).astype(np.int64)


def pack_weight(w):
    k, n = w.shape
    w = f64(np.asarray(w, np.float32).astype(ml_dtypes.bfloat16)).reshape(k // 32, 32, n)
    amax = np.abs(w).max(1)
    byte = np.clip(np.where(amax > 0, np.frexp(amax)[1] - 1 + 127 - 7, 1), 1, 254)
    scaled = (w * np.exp2(127.0 - byte)[:, None, :]).reshape(k, n).astype(np.float32)
    words = np.ascontiguousarray(scaled.reshape(k // 512, 128, 4, n).transpose(0, 1, 3, 2)).astype(ml_dtypes.float8_e4m3fn).view(np.uint8)
    return words, np.ascontiguousarray(byte.astype(np.uint8).reshape(k // 512, 16, n))


def unpack_weight(words, scales):
    g, p, n, _ = words.shape
    vals = np.ascontiguousarray(words).view(ml_dtypes.float8_e4m3fn).astype(np.float64) * np.repeat(np.exp2(scales.astype(np.float64) - 127.0), 8, axis=1)[..., None]
    return vals.transpose(0, 1, 3, 2).reshape(g * 512, n)


E2M1 = np.array([0.0, 0.5, 1.0, 1.5, 2.0, 3.0, 4.0, 6.0, -0.0, -0.5, -1.0, -1.5, -2.0, -3.0, -4.0, -6.0])


def pack_fp4(w):
    k, n = w.shape
    w = f64(np.asarray(w, np.float32).astype(ml_dtypes.bfloat16)).reshape(k // 32, 32, n)
    amax = np.abs(w).max(1)
    mant, ex = np.frexp(amax / 6.0)
    byte = np.clip(np.where(amax > 0, np.where(mant > 0.5, ex, ex - 1) + 127, 1), 1, 254)
    scaled = (w * np.exp2(127.0 - byte)[:, None, :]).reshape(k, n).astype(np.float32)
    c = np.ascontiguousarray(scaled.reshape(k // 512, 128, 4, n).transpose(0, 1, 3, 2)).astype(ml_dtypes.float4_e2m1fn).view(np.uint8) & 0xF
    words = (c[..., 0::2] | (c[..., 1::2] << 4)).reshape(k // 512, 128, 2 * n)
    return np.ascontiguousarray(words), np.ascontiguousarray(byte.astype(np.uint8).reshape(k // 512, 16, n))


def unpack_fp4(words, scales):
    g, _, n = scales.shape
    words = np.ascontiguousarray(words).reshape(g, 128, n, 2)
    nib = np.empty((g, 128, n, 4), np.uint8)
    nib[..., 0::2] = words & 0xF
    nib[..., 1::2] = words >> 4
    vals = E2M1[nib] * np.repeat(np.exp2(scales.astype(np.float64) - 127.0), 8, axis=1)[..., None]
    return vals.transpose(0, 1, 3, 2).reshape(g * 512, n)


K, T, S, N, H = 1024, 2048, 512, 128, 512


def setup_inputs():
    n = np.random.standard_normal
    s = mx_kscale(K)[:, None]
    u = mx_kscale(H)
    packed_xT = pack_weight(n((K, T)) * s)
    packed_w1 = pack_fp4(n((K, H)) / np.sqrt(K) / s)
    packed_w2 = pack_fp4(n((H, N)) / np.sqrt(H) / u[:, None])
    return {
        "x_words": packed_xT[0],
        "x_scales": packed_xT[1],
        "w1_words": packed_w1[0],
        "w1_scales": packed_w1[1],
        "unit": (np.random.uniform(0.6, 1.4, (H, 1)) * u[:, None]).astype(np.float32),
        "w2_words": packed_w2[0],
        "w2_scales": packed_w2[1],
        "offs": striped(np.random.permutation(T)[:S]),
        "h2": striped(np.random.permutation(S)),
        "h3": striped(np.random.permutation(S)),
    }


def reference(x_words, x_scales, w1_words, w1_scales, unit, w2_words, w2_scales, offs, h2, h3):
    xq = unpack_weight(x_words, x_scales)[:, unstriped(offs)]
    y = unpack_fp4(w1_words, w1_scales).T @ xq
    mag = np.abs(y)
    m2 = mag[:, unstriped(h2)]
    gm = np.sqrt(mag * m2 + 0.05)
    m3 = mag[:, unstriped(h3)]
    sal = gm - (0.4 * m3)
    s2 = sal[:, unstriped(h2)]
    lm = np.log(mag + 0.2)
    l2 = lm[:, unstriped(h2)]
    l3 = lm[:, unstriped(h3)]
    hps = lm + l2 + 0.7 * l3
    hid = f64(unit) * (s2 + hps)
    return unpack_fp4(w2_words, w2_scales).T @ mxq(hid, 0, "e4m3")

@@ -1,0 +1,204 @@
+from contextlib import ExitStack
+
+import concourse.mybir as mybir
+
+K, T, S, N, H = 1024, 2048, 512, 128, 512
+FLOPS = 2 * K * H * S + 2 * H * N * S
+
+F32 = mybir.dt.float32
+BF16 = mybir.dt.bfloat16
+I32 = mybir.dt.int32
+U32 = mybir.dt.uint32
+U16 = mybir.dt.uint16
+U8 = mybir.dt.uint8
+FP8X4 = mybir.dt.float8_e4m3fn_x4
+FP4X4 = mybir.dt.float4_e2m1fn_x4
+ACT = mybir.ActivationFunctionType
+ALU = mybir.AluOpType
+
+P = 128
+PACK = 4
+PASSES = K // (P * PACK)
+QUADS = 4
+MAG_WINDOW = 704
+CHUNKS = [(0, 256), (256, 384), (384, 512)]
+VECTOR_THIRDS = 2
+SCALAR_SECONDS = 2
+
+
+def load_scale_rows(queues, plane, scales):
+    for q in range(QUADS):
+        queues[q].dma_start(
+            out=plane[32 * q : 32 * q + 4, :, :].bitcast(I32),
+            in_=scales[:, 4 * q : 4 * q + 4, :].bitcast(I32).rearrange("o r c -> r o c"),
+        )
+
+
+def tile_picked_yhpspc_sec_p_kernel(tc, x_words, x_scales, w1_words, w1_scales, unit, w2_words, w2_scales, offs, h2, h3, out):
+    nc = tc.nc
+    with ExitStack() as ctx:
+        lists = ctx.enter_context(tc.tile_pool(name="lists", bufs=1))
+        keep = ctx.enter_context(tc.tile_pool(name="keep", bufs=1))
+        psum = ctx.enter_context(tc.psum_pool(name="psum", bufs=1))
+
+        offs_sb = lists.tile([P, S // 16], U16, name="offs_sb")
+        h2_sb = lists.tile([P, S // 16], U16, name="h2_sb")
+        h3_sb = lists.tile([P, S // 16], U16, name="h3_sb")
+
+        xs_table = keep.tile([P, PASSES, T], U8, name="xs_table", align_bytes=64)
+        w1s_raw = keep.tile([P, PASSES, H], U8, name="w1s_raw", tag="weight_scales", align_bytes=64)
+        nc.vector.memset(xs_table[:].bitcast(I32), 0)
+        nc.gpsimd.memset(w1s_raw[:].bitcast(I32), 0)
+        mag = [keep.tile([P, MAG_WINDOW], F32, name=f"mag{t}") for t in range(PACK)]
+        for t in range(PACK):
+            nc.vector.memset(mag[t][:, S:], 0.0)
+
+        w1_raw = keep.tile([P, PASSES, 2 * H], U8, name="w1_raw", tag="weight_words", align_bytes=64)
+        x_table = [keep.tile([P, T], I32, name=f"x_table{o}") for o in range(PASSES)]
+        unit_sb = keep.tile([P, PACK], F32, name="unit_sb")
+
+        nc.sync.dma_start(offs_sb[:], offs)
+        nc.sync.dma_start(h2_sb[:], h2)
+        nc.sync.dma_start(h3_sb[:], h3)
+        load_scale_rows([nc.scalar] * 4, xs_table, x_scales)
+        nc.scalar.dma_start(out=w1_raw[:].bitcast(I32), in_=w1_words.bitcast(I32).rearrange("o p c -> p o c"))
+        for o in range(PASSES):
+            nc.sync.dma_start(out=x_table[o][:], in_=x_words[o].rearrange("p n t -> p (n t)").bitcast(I32))
+        load_scale_rows([nc.scalar, nc.scalar, nc.gpsimd, nc.gpsimd], w1s_raw, w1_scales)
+        nc.gpsimd.dma_start(out=unit_sb[:], in_=unit.rearrange("(p t) o -> p (t o)", t=PACK))
+
+        w1w = keep.tile([P, PASSES, PACK, 2 * P], U8, name="w1w", align_bytes=64)
+        w1s = keep.tile([P, PASSES, PACK, P], U8, name="w1s", align_bytes=64)
+        xs = keep.tile([P, PASSES, S], U8, name="xs", align_bytes=64)
+        xw = [keep.tile([P, S], U32, name=f"xw{o}", align_bytes=64) for o in range(PASSES)]
+        nc.vector.tensor_copy(
+            out=w1w[:].bitcast(U16),
+            in_=w1_raw[:].bitcast(U16).rearrange("p o (m t) -> p o t m", t=PACK),
+        )
+        for o in range(PASSES):
+            nc.vector.tensor_copy(out=xs[:, o, :], in_=xs_table[:, o, :].indirect(offs_sb[:]))
+        nc.vector.tensor_copy(out=w1s[:], in_=w1s_raw[:].rearrange("p o (m t) -> p o t m", t=PACK))
+        for o in range(PASSES):
+            nc.vector.tensor_copy(out=xw[o][:], in_=x_table[o][:].bitcast(U32).indirect(offs_sb[:]))
+
+        w2w = keep.tile([P, 2 * N], U8, name="w2w", tag="weight_words", align_bytes=64)
+        w2s = keep.tile([P, 1, N], U8, name="w2s", tag="weight_scales", align_bytes=64)
+        nc.gpsimd.memset(w2s[:].bitcast(I32), 0)
+        nc.sync.dma_start(out=w2w[:].bitcast(I32), in_=w2_words[0].bitcast(I32))
+        load_scale_rows([nc.sync] * 4, w2s, w2_scales)
+
+        unit7 = keep.tile([P, PACK], F32, name="unit7")
+        unit4 = keep.tile([P, PACK], F32, name="unit4")
+        nc.gpsimd.tensor_scalar(unit7[:], unit_sb[:], 0.7, 0.0, ALU.mult, ALU.add)
+        nc.gpsimd.tensor_scalar(unit4[:], unit_sb[:], -0.4, 0.0, ALU.mult, ALU.add)
+
+        y = [psum.tile([P, S], F32, name=f"y{t}") for t in range(PACK)]
+        for t in range(PACK):
+            for o in range(PASSES):
+                nc.tensor.matmul_mx(
+                    out=y[t][:],
+                    lhsT=w1w[:, o, t, :].bitcast(FP4X4),
+                    lhsT_scale=w1s[:, o, t, :],
+                    rhs=xw[o][:].bitcast(FP8X4),
+                    rhs_scale=xs[:, o, :],
+                    start=(o == 0),
+                    stop=(o == PASSES - 1),
+                )
+
+        for t in range(PACK):
+            nc.scalar.activation(mag[t][:, :S], y[t][:], ACT.Abs)
+
+        mag_again = keep.tile([P, PACK, S], F32, name="mag_again")
+        for t in range(PACK):
+            nc.sync.dma_start(out=mag_again[:, t, :], in_=mag[t][:, :S])
+
+        m3 = keep.tile([P, PACK, S], F32, name="m3")
+        prod = keep.tile([P, PACK, S], F32, name="prod")
+        lm = keep.tile([P, PACK, S], F32, name="lm")
+        l3 = keep.tile([P, PACK, S], F32, name="l3")
+        for t in range(VECTOR_THIRDS):
+            nc.vector.tensor_copy(m3[:, t, :], mag[t][:].indirect(h3_sb[:]))
+        for t in range(PACK):
+            nc.vector.tensor_tensor(prod[:, t, :], mag[t][:].indirect(h2_sb[:]), mag_again[:, t, :], ALU.mult)
+        for t in range(PACK):
+            nc.scalar.activation(lm[:, t, :], mag[t][:, :S], ACT.Ln, bias=0.2)
+        for t in range(VECTOR_THIRDS, PACK):
+            nc.scalar.activation(m3[:, t, :], mag[t][:].indirect(h3_sb[:]), ACT.Copy)
+        for t in range(PACK):
+            nc.scalar.activation(l3[:, t, :], m3[:, t, :], ACT.Ln, bias=0.2)
+
+        lmu = keep.tile([P, PACK, S], F32, name="lmu")
+        stay = keep.tile([P, PACK, S], F32, name="stay")
+        part = keep.tile([P, PACK, S], F32, name="part")
+        for t in range(PACK):
+            nc.vector.tensor_scalar(lmu[:, t, :], lm[:, t, :], unit_sb[:, t : t + 1], None, ALU.mult)
+        for t in range(PACK):
+            nc.vector.scalar_tensor_tensor(
+                part[:, t, :], m3[:, t, :], unit4[:, t : t + 1], lmu[:, t, :], ALU.mult, ALU.add
+            )
+        for t in range(PACK):
+            nc.vector.scalar_tensor_tensor(
+                stay[:, t, :], l3[:, t, :], unit7[:, t : t + 1], lmu[:, t, :], ALU.mult, ALU.add
+            )
+
+        gm = keep.tile([P, PACK, S], F32, name="gm")
+        fetch = [keep.tile([P, S], F32, name=f"fetch{t}") for t in range(PACK)]
+        fetched = keep.tile([P, SCALAR_SECONDS, S], F32, name="fetched")
+        for t in range(PACK):
+            nc.scalar.activation(gm[:, t, :], prod[:, t, :], ACT.Sqrt, bias=0.05)
+        for t in range(PACK):
+            nc.vector.scalar_tensor_tensor(
+                fetch[t][:], gm[:, t, :], unit_sb[:, t : t + 1], part[:, t, :], ALU.mult, ALU.add
+            )
+        for half in range(2):
+            for t in range(SCALAR_SECONDS):
+                nc.scalar.activation(
+                    fetched[:, t, half * 256 : (half + 1) * 256],
+                    fetch[t][:].indirect(h2_sb[:, half * 16 : (half + 1) * 16]),
+                    ACT.Copy,
+                )
+
+        hid = [keep.tile([P, PACK, c1 - c0], F32, name=f"hid{c0}") for c0, c1 in CHUNKS]
+
+        def second_harmonic(c):
+            c0, c1 = CHUNKS[c]
+            for t in range(SCALAR_SECONDS, PACK):
+                nc.vector.tensor_tensor(
+                    hid[c][:, t, :], fetch[t][:].indirect(h2_sb[:, c0 // 16 : c1 // 16]), stay[:, t, c0:c1], ALU.add
+                )
+            nc.vector.tensor_tensor(
+                hid[c][:, :SCALAR_SECONDS, :], fetched[:, :, c0:c1], stay[:, :SCALAR_SECONDS, c0:c1], ALU.add
+            )
+
+        def finish(c, interleave):
+            c0, c1 = CHUNKS[c]
+            width = c1 - c0
+            grouped = keep.tile([P, width, PACK], BF16, name=f"grouped{c}", align_bytes=64)
+            codes = keep.tile([P, width], U32, name=f"codes{c}", align_bytes=64)
+            scales = keep.tile([P, width], U8, name=f"scales{c}", align_bytes=64)
+            interleave(
+                grouped[:].rearrange("p (c i) t -> p c t i", i=4),
+                hid[c][:].rearrange("p t (c i) -> p c t i", i=4),
+            )
+            nc.vector.quantize_mx(
+                out=codes[:].bitcast(FP8X4), scales=scales[:], in_=grouped[:].rearrange("p j t -> p (j t)")
+            )
+            acc = psum.tile([P, width], F32, name=f"acc{c}")
+            nc.tensor.matmul_mx(
+                out=acc[:],
+                lhsT=w2w[:].bitcast(FP4X4),
+                lhsT_scale=w2s[:, 0, :],
+                rhs=codes[:].bitcast(FP8X4),
+                rhs_scale=scales[:],
+                start=True,
+                stop=True,
+            )
+            result = keep.tile([P, width], F32, name=f"result{c}")
+            nc.scalar.copy(result[:], acc[:])
+            nc.sync.dma_start(out=out[:, c0:c1], in_=result[:])
+
+        second_harmonic(0)
+        for c in range(1, len(CHUNKS)):
+            second_harmonic(c)
+            finish(c - 1, nc.scalar.copy)
+        finish(len(CHUNKS) - 1, nc.vector.tensor_copy)

@@ -22,8 +22,7 @@ PASSES = K // (P * PACK)
 QUADS = 4
 MAG_WINDOW = 704
 CHUNKS = [(0, 256), (256, 384), (384, 512)]
-VECTOR_THIRDS = 2
-SCALAR_SECONDS = 2
+VECTOR_THIRDS = 1
 
 
 def load_scale_rows(queues, plane, scales):
@@ -45,7 +44,7 @@ def tile_picked_yhpspc_sec_p_kernel(tc, x_words, x_scales, w1_words, w1_scales, 
         h2_sb = lists.tile([P, S // 16], U16, name="h2_sb")
         h3_sb = lists.tile([P, S // 16], U16, name="h3_sb")
 
-        xs_table = keep.tile([P, PASSES, T], U8, name="xs_table", align_bytes=64)
+        xs_table = keep.tile([P, PASSES, T], U8, name="xs_table", tag="scale_rows", align_bytes=64)
         w1s_raw = keep.tile([P, PASSES, H], U8, name="w1s_raw", tag="weight_scales", align_bytes=64)
         nc.vector.memset(xs_table[:].bitcast(I32), 0)
         nc.gpsimd.memset(w1s_raw[:].bitcast(I32), 0)
@@ -54,7 +53,7 @@ def tile_picked_yhpspc_sec_p_kernel(tc, x_words, x_scales, w1_words, w1_scales, 
             nc.vector.memset(mag[t][:, S:], 0.0)
 
         w1_raw = keep.tile([P, PASSES, 2 * H], U8, name="w1_raw", tag="weight_words", align_bytes=64)
-        x_table = [keep.tile([P, T], I32, name=f"x_table{o}") for o in range(PASSES)]
+        x_first = keep.tile([P, T], I32, name="x_first", align_bytes=64)
         unit_sb = keep.tile([P, PACK], F32, name="unit_sb")
 
         nc.sync.dma_start(offs_sb[:], offs)
@@ -62,27 +61,32 @@ def tile_picked_yhpspc_sec_p_kernel(tc, x_words, x_scales, w1_words, w1_scales, 
         nc.sync.dma_start(h3_sb[:], h3)
         load_scale_rows([nc.scalar] * 4, xs_table, x_scales)
         nc.scalar.dma_start(out=w1_raw[:].bitcast(I32), in_=w1_words.bitcast(I32).rearrange("o p c -> p o c"))
-        for o in range(PASSES):
-            nc.sync.dma_start(out=x_table[o][:], in_=x_words[o].rearrange("p n t -> p (n t)").bitcast(I32))
-        load_scale_rows([nc.scalar, nc.scalar, nc.gpsimd, nc.gpsimd], w1s_raw, w1_scales)
+        nc.sync.dma_start(out=x_first[:], in_=x_words[0].rearrange("p n t -> p (n t)").bitcast(I32))
+        load_scale_rows([nc.scalar, nc.scalar, nc.scalar, nc.gpsimd], w1s_raw, w1_scales)
         nc.gpsimd.dma_start(out=unit_sb[:], in_=unit.rearrange("(p t) o -> p (t o)", t=PACK))
 
         w1w = keep.tile([P, PASSES, PACK, 2 * P], U8, name="w1w", align_bytes=64)
         w1s = keep.tile([P, PASSES, PACK, P], U8, name="w1s", align_bytes=64)
         xs = keep.tile([P, PASSES, S], U8, name="xs", align_bytes=64)
-        xw = [keep.tile([P, S], U32, name=f"xw{o}", align_bytes=64) for o in range(PASSES)]
+        xw = [keep.tile([P, S], U32, name="xw0", align_bytes=64)]
         nc.vector.tensor_copy(
             out=w1w[:].bitcast(U16),
             in_=w1_raw[:].bitcast(U16).rearrange("p o (m t) -> p o t m", t=PACK),
         )
+        x_second = keep.tile([P, T], I32, name="x_second", tag="weight_words", align_bytes=64)
+        nc.sync.dma_start(out=x_second[:], in_=x_words[1].rearrange("p n t -> p (n t)").bitcast(I32))
+        x_table = [x_first, x_second]
+        nc.vector.tensor_copy(out=xw[0][:], in_=x_table[0][:].bitcast(U32).indirect(offs_sb[:]))
         for o in range(PASSES):
             nc.vector.tensor_copy(out=xs[:, o, :], in_=xs_table[:, o, :].indirect(offs_sb[:]))
         nc.vector.tensor_copy(out=w1s[:], in_=w1s_raw[:].rearrange("p o (m t) -> p o t m", t=PACK))
-        for o in range(PASSES):
-            nc.vector.tensor_copy(out=xw[o][:], in_=x_table[o][:].bitcast(U32).indirect(offs_sb[:]))
+        xw.append(keep.tile([P, S], U32, name="xw1", tag="weight_scales", align_bytes=64))
+        nc.vector.tensor_copy(out=xw[1][:], in_=x_table[1][:].bitcast(U32).indirect(offs_sb[:]))
+        warm = keep.tile([P, 1], F32, name="warm")
+        nc.scalar.activation(warm[:], unit_sb[:, 0:1], ACT.Ln, bias=0.2, scale=0.0)
 
         w2w = keep.tile([P, 2 * N], U8, name="w2w", tag="weight_words", align_bytes=64)
-        w2s = keep.tile([P, 1, N], U8, name="w2s", tag="weight_scales", align_bytes=64)
+        w2s = keep.tile([P, 1, N], U8, name="w2s", tag="scale_rows", align_bytes=64)
         nc.gpsimd.memset(w2s[:].bitcast(I32), 0)
         nc.sync.dma_start(out=w2w[:].bitcast(I32), in_=w2_words[0].bitcast(I32))
         load_scale_rows([nc.sync] * 4, w2s, w2_scales)
@@ -108,18 +112,21 @@ def tile_picked_yhpspc_sec_p_kernel(tc, x_words, x_scales, w1_words, w1_scales, 
         for t in range(PACK):
             nc.scalar.activation(mag[t][:, :S], y[t][:], ACT.Abs)
 
-        mag_again = keep.tile([P, PACK, S], F32, name="mag_again")
-        for t in range(PACK):
-            nc.sync.dma_start(out=mag_again[:, t, :], in_=mag[t][:, :S])
+        mag_again = keep.tile([P, PACK - 1, S], F32, name="mag_again")
+        for t in range(1, PACK):
+            nc.sync.dma_start(out=mag_again[:, t - 1, :], in_=mag[t][:, :S])
 
+        m2 = keep.tile([P, S], F32, name="m2")
         m3 = keep.tile([P, PACK, S], F32, name="m3")
         prod = keep.tile([P, PACK, S], F32, name="prod")
         lm = keep.tile([P, PACK, S], F32, name="lm")
         l3 = keep.tile([P, PACK, S], F32, name="l3")
+        nc.vector.tensor_copy(m2[:], mag[0][:].indirect(h2_sb[:]))
         for t in range(VECTOR_THIRDS):
             nc.vector.tensor_copy(m3[:, t, :], mag[t][:].indirect(h3_sb[:]))
-        for t in range(PACK):
-            nc.vector.tensor_tensor(prod[:, t, :], mag[t][:].indirect(h2_sb[:]), mag_again[:, t, :], ALU.mult)
+        nc.vector.tensor_tensor(prod[:, 0, :], m2[:], mag[0][:, :S], ALU.mult)
+        for t in range(1, PACK):
+            nc.vector.tensor_tensor(prod[:, t, :], mag[t][:].indirect(h2_sb[:]), mag_again[:, t - 1, :], ALU.mult)
         for t in range(PACK):
             nc.scalar.activation(lm[:, t, :], mag[t][:, :S], ACT.Ln, bias=0.2)
         for t in range(VECTOR_THIRDS, PACK):
@@ -136,49 +143,39 @@ def tile_picked_yhpspc_sec_p_kernel(tc, x_words, x_scales, w1_words, w1_scales, 
             nc.vector.scalar_tensor_tensor(
                 part[:, t, :], m3[:, t, :], unit4[:, t : t + 1], lmu[:, t, :], ALU.mult, ALU.add
             )
-        for t in range(PACK):
-            nc.vector.scalar_tensor_tensor(
-                stay[:, t, :], l3[:, t, :], unit7[:, t : t + 1], lmu[:, t, :], ALU.mult, ALU.add
-            )
 
         gm = keep.tile([P, PACK, S], F32, name="gm")
         fetch = [keep.tile([P, S], F32, name=f"fetch{t}") for t in range(PACK)]
-        fetched = keep.tile([P, SCALAR_SECONDS, S], F32, name="fetched")
         for t in range(PACK):
             nc.scalar.activation(gm[:, t, :], prod[:, t, :], ACT.Sqrt, bias=0.05)
         for t in range(PACK):
             nc.vector.scalar_tensor_tensor(
                 fetch[t][:], gm[:, t, :], unit_sb[:, t : t + 1], part[:, t, :], ALU.mult, ALU.add
             )
-        for half in range(2):
-            for t in range(SCALAR_SECONDS):
-                nc.scalar.activation(
-                    fetched[:, t, half * 256 : (half + 1) * 256],
-                    fetch[t][:].indirect(h2_sb[:, half * 16 : (half + 1) * 16]),
-                    ACT.Copy,
-                )
-
-        hid = [keep.tile([P, PACK, c1 - c0], F32, name=f"hid{c0}") for c0, c1 in CHUNKS]
-
-        def second_harmonic(c):
-            c0, c1 = CHUNKS[c]
-            for t in range(SCALAR_SECONDS, PACK):
-                nc.vector.tensor_tensor(
-                    hid[c][:, t, :], fetch[t][:].indirect(h2_sb[:, c0 // 16 : c1 // 16]), stay[:, t, c0:c1], ALU.add
-                )
-            nc.vector.tensor_tensor(
-                hid[c][:, :SCALAR_SECONDS, :], fetched[:, :, c0:c1], stay[:, :SCALAR_SECONDS, c0:c1], ALU.add
+        for t in range(PACK):
+            nc.vector.scalar_tensor_tensor(
+                stay[:, t, :], l3[:, t, :], unit7[:, t : t + 1], lmu[:, t, :], ALU.mult, ALU.add
             )
 
-        def finish(c, interleave):
-            c0, c1 = CHUNKS[c]
+        fetched = [keep.tile([P, PACK, c1 - c0], F32, name=f"fetched{c0}") for c0, c1 in CHUNKS]
+        for c, (c0, c1) in enumerate(CHUNKS):
+            for t in range(PACK):
+                window = fetch[t][:].indirect(h2_sb[:, c0 // 16 : c1 // 16])
+                if c == 0 and t == PACK - 1:
+                    nc.vector.tensor_copy(fetched[c][:, t, :], window)
+                else:
+                    nc.scalar.activation(fetched[c][:, t, :], window, ACT.Copy)
+
+        for c, (c0, c1) in enumerate(CHUNKS):
             width = c1 - c0
             grouped = keep.tile([P, width, PACK], BF16, name=f"grouped{c}", align_bytes=64)
             codes = keep.tile([P, width], U32, name=f"codes{c}", align_bytes=64)
             scales = keep.tile([P, width], U8, name=f"scales{c}", align_bytes=64)
-            interleave(
+            nc.vector.tensor_tensor(
                 grouped[:].rearrange("p (c i) t -> p c t i", i=4),
-                hid[c][:].rearrange("p t (c i) -> p c t i", i=4),
+                fetched[c][:].rearrange("p t (c i) -> p c t i", i=4),
+                stay[:, :, c0:c1].rearrange("p t (c i) -> p c t i", i=4),
+                ALU.add,
             )
             nc.vector.quantize_mx(
                 out=codes[:].bitcast(FP8X4), scales=scales[:], in_=grouped[:].rearrange("p j t -> p (j t)")
@@ -196,9 +193,3 @@ def tile_picked_yhpspc_sec_p_kernel(tc, x_words, x_scales, w1_words, w1_scales, 
             result = keep.tile([P, width], F32, name=f"result{c}")
             nc.scalar.copy(result[:], acc[:])
             nc.sync.dma_start(out=out[:, c0:c1], in_=result[:])
-
-        second_harmonic(0)
-        for c in range(1, len(CHUNKS)):
-            second_harmonic(c)
-            finish(c - 1, nc.scalar.copy)
-        finish(len(CHUNKS) - 1, nc.vector.tensor_copy)

@@ -47,7 +47,7 @@ def tile_picked_yhpspc_sec_p_kernel(tc, x_words, x_scales, w1_words, w1_scales, 
         xs_table = keep.tile([P, PASSES, T], U8, name="xs_table", tag="scale_rows", align_bytes=64)
         w1s_raw = keep.tile([P, PASSES, H], U8, name="w1s_raw", tag="weight_scales", align_bytes=64)
         nc.vector.memset(xs_table[:].bitcast(I32), 0)
-        nc.gpsimd.memset(w1s_raw[:].bitcast(I32), 0)
+        nc.vector.memset(w1s_raw[:].bitcast(I32), 0)
         mag = [keep.tile([P, MAG_WINDOW], F32, name=f"mag{t}") for t in range(PACK)]
         for t in range(PACK):
             nc.vector.memset(mag[t][:, S:], 0.0)
@@ -60,9 +60,9 @@ def tile_picked_yhpspc_sec_p_kernel(tc, x_words, x_scales, w1_words, w1_scales, 
         nc.sync.dma_start(h2_sb[:], h2)
         nc.sync.dma_start(h3_sb[:], h3)
         load_scale_rows([nc.scalar] * 4, xs_table, x_scales)
-        nc.scalar.dma_start(out=w1_raw[:].bitcast(I32), in_=w1_words.bitcast(I32).rearrange("o p c -> p o c"))
-        nc.sync.dma_start(out=x_first[:], in_=x_words[0].rearrange("p n t -> p (n t)").bitcast(I32))
-        load_scale_rows([nc.scalar, nc.scalar, nc.scalar, nc.gpsimd], w1s_raw, w1_scales)
+        nc.sync.dma_start(out=w1_raw[:].bitcast(I32), in_=w1_words.bitcast(I32).rearrange("o p c -> p o c"))
+        nc.sync.dma_start(out=x_first[:], in_=x_words[0].rearrange("p n t -> p (n t)").bitcast(I32), max_dma_last_dim=4096)
+        load_scale_rows([nc.scalar, nc.scalar, nc.gpsimd, nc.gpsimd], w1s_raw, w1_scales)
         nc.gpsimd.dma_start(out=unit_sb[:], in_=unit.rearrange("(p t) o -> p (t o)", t=PACK))
 
         w1w = keep.tile([P, PASSES, PACK, 2 * P], U8, name="w1w", align_bytes=64)
@@ -74,7 +74,7 @@ def tile_picked_yhpspc_sec_p_kernel(tc, x_words, x_scales, w1_words, w1_scales, 
             in_=w1_raw[:].bitcast(U16).rearrange("p o (m t) -> p o t m", t=PACK),
         )
         x_second = keep.tile([P, T], I32, name="x_second", tag="weight_words", align_bytes=64)
-        nc.sync.dma_start(out=x_second[:], in_=x_words[1].rearrange("p n t -> p (n t)").bitcast(I32))
+        nc.sync.dma_start(out=x_second[:], in_=x_words[1].rearrange("p n t -> p (n t)").bitcast(I32), max_dma_last_dim=4096)
         x_table = [x_first, x_second]
         nc.vector.tensor_copy(out=xw[0][:], in_=x_table[0][:].bitcast(U32).indirect(offs_sb[:]))
         for o in range(PASSES):
@@ -171,11 +171,16 @@ def tile_picked_yhpspc_sec_p_kernel(tc, x_words, x_scales, w1_words, w1_scales, 
             grouped = keep.tile([P, width, PACK], BF16, name=f"grouped{c}", align_bytes=64)
             codes = keep.tile([P, width], U32, name=f"codes{c}", align_bytes=64)
             scales = keep.tile([P, width], U8, name=f"scales{c}", align_bytes=64)
+            pairs = keep.tile([P, 2, width, 2], BF16, name=f"pairs{c}", align_bytes=64)
             nc.vector.tensor_tensor(
-                grouped[:].rearrange("p (c i) t -> p c t i", i=4),
-                fetched[c][:].rearrange("p t (c i) -> p c t i", i=4),
-                stay[:, :, c0:c1].rearrange("p t (c i) -> p c t i", i=4),
+                pairs[:],
+                fetched[c][:].rearrange("p (u e) j -> p u j e", e=2),
+                stay[:, :, c0:c1].rearrange("p (u e) j -> p u j e", e=2),
                 ALU.add,
+            )
+            nc.vector.tensor_copy(
+                grouped[:].bitcast(I32),
+                pairs[:].rearrange("p u j e -> p u (j e)").bitcast(I32).rearrange("p u j -> p j u"),
             )
             nc.vector.quantize_mx(
                 out=codes[:].bitcast(FP8X4), scales=scales[:], in_=grouped[:].rearrange("p j t -> p (j t)")

@@ -23,6 +23,7 @@ QUADS = 4
 MAG_WINDOW = 704
 CHUNKS = [(0, 256), (256, 384), (384, 512)]
 VECTOR_THIRDS = 1
+HALVES = [(0, S // 2), (S // 2, S)]
 
 
 def load_scale_rows(queues, plane, scales):
@@ -44,30 +45,34 @@ def tile_picked_yhpspc_sec_p_kernel(tc, x_words, x_scales, w1_words, w1_scales, 
         h2_sb = lists.tile([P, S // 16], U16, name="h2_sb")
         h3_sb = lists.tile([P, S // 16], U16, name="h3_sb")
 
-        xs_table = keep.tile([P, PASSES, T], U8, name="xs_table", tag="scale_rows", align_bytes=64)
+        xs_table = keep.tile([P, T], U8, name="xs_table", tag="scale_rows", align_bytes=64)
         w1s_raw = keep.tile([P, PASSES, H], U8, name="w1s_raw", tag="weight_scales", align_bytes=64)
         nc.vector.memset(xs_table[:].bitcast(I32), 0)
-        nc.vector.memset(w1s_raw[:].bitcast(I32), 0)
+        nc.gpsimd.memset(w1s_raw[:].bitcast(I32), 0)
         mag = [keep.tile([P, MAG_WINDOW], F32, name=f"mag{t}") for t in range(PACK)]
         for t in range(PACK):
             nc.vector.memset(mag[t][:, S:], 0.0)
 
         w1_raw = keep.tile([P, PASSES, 2 * H], U8, name="w1_raw", tag="weight_words", align_bytes=64)
-        x_first = keep.tile([P, T], I32, name="x_first", align_bytes=64)
+        x_first = keep.tile([P, T], I32, name="x_first", tag="first_words", align_bytes=64)
         unit_sb = keep.tile([P, PACK], F32, name="unit_sb")
 
         nc.sync.dma_start(offs_sb[:], offs)
+        nc.sync.dma_start(out=w1_raw[:].bitcast(I32), in_=w1_words.bitcast(I32).rearrange("o p c -> p o c"))
         nc.sync.dma_start(h2_sb[:], h2)
         nc.sync.dma_start(h3_sb[:], h3)
-        load_scale_rows([nc.scalar] * 4, xs_table, x_scales)
-        nc.sync.dma_start(out=w1_raw[:].bitcast(I32), in_=w1_words.bitcast(I32).rearrange("o p c -> p o c"))
+        for r in range(4):
+            nc.scalar.dma_start(
+                out=xs_table[r:P:16, :].bitcast(I32),
+                in_=x_scales[:, r:16:4, :].bitcast(I32).rearrange("o q c -> q o c"),
+            )
         nc.sync.dma_start(out=x_first[:], in_=x_words[0].rearrange("p n t -> p (n t)").bitcast(I32), max_dma_last_dim=4096)
-        load_scale_rows([nc.scalar, nc.scalar, nc.gpsimd, nc.gpsimd], w1s_raw, w1_scales)
+        load_scale_rows([nc.gpsimd] * 4, w1s_raw, w1_scales)
+        xs = [keep.tile([P, S], U8, name=f"xs{o}", align_bytes=64) for o in range(PASSES)]
+        nc.gpsimd.memset(xs[1][:].bitcast(I32), 0)
         nc.gpsimd.dma_start(out=unit_sb[:], in_=unit.rearrange("(p t) o -> p (t o)", t=PACK))
 
         w1w = keep.tile([P, PASSES, PACK, 2 * P], U8, name="w1w", align_bytes=64)
-        w1s = keep.tile([P, PASSES, PACK, P], U8, name="w1s", align_bytes=64)
-        xs = keep.tile([P, PASSES, S], U8, name="xs", align_bytes=64)
         xw = [keep.tile([P, S], U32, name="xw0", align_bytes=64)]
         nc.vector.tensor_copy(
             out=w1w[:].bitcast(U16),
@@ -76,14 +81,21 @@ def tile_picked_yhpspc_sec_p_kernel(tc, x_words, x_scales, w1_words, w1_scales, 
         x_second = keep.tile([P, T], I32, name="x_second", tag="weight_words", align_bytes=64)
         nc.sync.dma_start(out=x_second[:], in_=x_words[1].rearrange("p n t -> p (n t)").bitcast(I32), max_dma_last_dim=4096)
         x_table = [x_first, x_second]
+        nc.vector.tensor_copy(out=xs[0][:], in_=xs_table[:].indirect(offs_sb[:]))
+        for q in range(QUADS):
+            nc.scalar.dma_start(
+                out=xs[1][32 * q : 32 * q + 4, :].bitcast(I32), in_=xs[0][32 * q + 16 : 32 * q + 20, :].bitcast(I32)
+            )
         nc.vector.tensor_copy(out=xw[0][:], in_=x_table[0][:].bitcast(U32).indirect(offs_sb[:]))
-        for o in range(PASSES):
-            nc.vector.tensor_copy(out=xs[:, o, :], in_=xs_table[:, o, :].indirect(offs_sb[:]))
+        w1s = keep.tile([P, PASSES, PACK, P], U8, name="w1s", tag="first_words", align_bytes=64)
         nc.vector.tensor_copy(out=w1s[:], in_=w1s_raw[:].rearrange("p o (m t) -> p o t m", t=PACK))
         xw.append(keep.tile([P, S], U32, name="xw1", tag="weight_scales", align_bytes=64))
-        nc.vector.tensor_copy(out=xw[1][:], in_=x_table[1][:].bitcast(U32).indirect(offs_sb[:]))
+        for c0, c1 in HALVES:
+            nc.vector.tensor_copy(
+                out=xw[1][:, c0:c1], in_=x_table[1][:].bitcast(U32).indirect(offs_sb[:, c0 // 16 : c1 // 16])
+            )
         warm = keep.tile([P, 1], F32, name="warm")
-        nc.scalar.activation(warm[:], unit_sb[:, 0:1], ACT.Ln, bias=0.2, scale=0.0)
+        nc.scalar.activation(warm[:], w1w[:, 0, 0, 0:4].bitcast(U32), ACT.Ln, bias=0.2, scale=0.0)
 
         w2w = keep.tile([P, 2 * N], U8, name="w2w", tag="weight_words", align_bytes=64)
         w2s = keep.tile([P, 1, N], U8, name="w2s", tag="scale_rows", align_bytes=64)
@@ -96,21 +108,20 @@ def tile_picked_yhpspc_sec_p_kernel(tc, x_words, x_scales, w1_words, w1_scales, 
         nc.gpsimd.tensor_scalar(unit7[:], unit_sb[:], 0.7, 0.0, ALU.mult, ALU.add)
         nc.gpsimd.tensor_scalar(unit4[:], unit_sb[:], -0.4, 0.0, ALU.mult, ALU.add)
 
-        y = [psum.tile([P, S], F32, name=f"y{t}") for t in range(PACK)]
         for t in range(PACK):
-            for o in range(PASSES):
-                nc.tensor.matmul_mx(
-                    out=y[t][:],
-                    lhsT=w1w[:, o, t, :].bitcast(FP4X4),
-                    lhsT_scale=w1s[:, o, t, :],
-                    rhs=xw[o][:].bitcast(FP8X4),
-                    rhs_scale=xs[:, o, :],
-                    start=(o == 0),
-                    stop=(o == PASSES - 1),
-                )
-
-        for t in range(PACK):
-            nc.scalar.activation(mag[t][:, :S], y[t][:], ACT.Abs)
+            for c0, c1 in HALVES if t == 0 else [(0, S)]:
+                y = psum.tile([P, c1 - c0], F32, name=f"y{t}_{c0}")
+                for o in range(PASSES):
+                    nc.tensor.matmul_mx(
+                        out=y[:],
+                        lhsT=w1w[:, o, t, :].bitcast(FP4X4),
+                        lhsT_scale=w1s[:, o, t, :],
+                        rhs=xw[o][:, c0:c1].bitcast(FP8X4),
+                        rhs_scale=xs[o][:, c0:c1],
+                        start=(o == 0),
+                        stop=(o == PASSES - 1),
+                    )
+                nc.scalar.activation(mag[t][:, c0:c1], y[:], ACT.Abs)
 
         mag_again = keep.tile([P, PACK - 1, S], F32, name="mag_again")
         for t in range(1, PACK):

@@ -17,13 +17,15 @@ ACT = mybir.ActivationFunctionType
 ALU = mybir.AluOpType
 
 P = 128
-PACK = 4
-PASSES = K // (P * PACK)
+SLOTS = 4
+PASSES = K // (P * SLOTS)
 QUADS = 4
+GROUP = 16
+SECOND_PASS_ROW = 16
 MAG_WINDOW = 704
-CHUNKS = [(0, 256), (256, 384), (384, 512)]
-VECTOR_THIRDS = 1
 HALVES = [(0, S // 2), (S // 2, S)]
+CHUNKS = [(0, 256), (256, 384), (384, 512)]
+LARGE_LOAD_PIECE = 4096
 
 
 def load_scale_rows(queues, plane, scales):
@@ -34,66 +36,82 @@ def load_scale_rows(queues, plane, scales):
         )
 
 
-def tile_picked_yhpspc_sec_p_kernel(tc, x_words, x_scales, w1_words, w1_scales, unit, w2_words, w2_scales, offs, h2, h3, out):
+def entries(list_tile, first, last):
+    return list_tile[:, first // GROUP : last // GROUP]
+
+
+def tile_picked_yhpspc_sec_p_kernel(
+    tc, x_words, x_scales, w1_words, w1_scales, unit, w2_words, w2_scales, offs, h2, h3, out
+):
     nc = tc.nc
     with ExitStack() as ctx:
         lists = ctx.enter_context(tc.tile_pool(name="lists", bufs=1))
         keep = ctx.enter_context(tc.tile_pool(name="keep", bufs=1))
         psum = ctx.enter_context(tc.psum_pool(name="psum", bufs=1))
 
-        offs_sb = lists.tile([P, S // 16], U16, name="offs_sb")
-        h2_sb = lists.tile([P, S // 16], U16, name="h2_sb")
-        h3_sb = lists.tile([P, S // 16], U16, name="h3_sb")
+        offs_sb = lists.tile([P, S // GROUP], U16, name="offs_sb")
+        h2_sb = lists.tile([P, S // GROUP], U16, name="h2_sb")
+        h3_sb = lists.tile([P, S // GROUP], U16, name="h3_sb")
 
         xs_table = keep.tile([P, T], U8, name="xs_table", tag="scale_rows", align_bytes=64)
         w1s_raw = keep.tile([P, PASSES, H], U8, name="w1s_raw", tag="weight_scales", align_bytes=64)
         nc.vector.memset(xs_table[:].bitcast(I32), 0)
         nc.gpsimd.memset(w1s_raw[:].bitcast(I32), 0)
-        mag = [keep.tile([P, MAG_WINDOW], F32, name=f"mag{t}") for t in range(PACK)]
-        for t in range(PACK):
+        mag = [keep.tile([P, MAG_WINDOW], F32, name=f"mag{t}") for t in range(SLOTS)]
+        for t in range(SLOTS):
             nc.vector.memset(mag[t][:, S:], 0.0)
 
         w1_raw = keep.tile([P, PASSES, 2 * H], U8, name="w1_raw", tag="weight_words", align_bytes=64)
-        x_first = keep.tile([P, T], I32, name="x_first", tag="first_words", align_bytes=64)
-        unit_sb = keep.tile([P, PACK], F32, name="unit_sb")
+        x_first = keep.tile([P, T], I32, name="x_first", align_bytes=64)
+        unit_sb = keep.tile([P, SLOTS], F32, name="unit_sb")
 
         nc.sync.dma_start(offs_sb[:], offs)
-        nc.sync.dma_start(out=w1_raw[:].bitcast(I32), in_=w1_words.bitcast(I32).rearrange("o p c -> p o c"))
+        nc.scalar.dma_start(out=w1_raw[:].bitcast(I32), in_=w1_words.bitcast(I32).rearrange("o p c -> p o c"))
         nc.sync.dma_start(h2_sb[:], h2)
         nc.sync.dma_start(h3_sb[:], h3)
         for r in range(4):
             nc.scalar.dma_start(
-                out=xs_table[r:P:16, :].bitcast(I32),
+                out=xs_table[r:P:SECOND_PASS_ROW, :].bitcast(I32),
                 in_=x_scales[:, r:16:4, :].bitcast(I32).rearrange("o q c -> q o c"),
             )
-        nc.sync.dma_start(out=x_first[:], in_=x_words[0].rearrange("p n t -> p (n t)").bitcast(I32), max_dma_last_dim=4096)
-        load_scale_rows([nc.gpsimd] * 4, w1s_raw, w1_scales)
-        xs = [keep.tile([P, S], U8, name=f"xs{o}", align_bytes=64) for o in range(PASSES)]
-        nc.gpsimd.memset(xs[1][:].bitcast(I32), 0)
-        nc.gpsimd.dma_start(out=unit_sb[:], in_=unit.rearrange("(p t) o -> p (t o)", t=PACK))
+        nc.sync.dma_start(
+            out=x_first[:],
+            in_=x_words[0].rearrange("p n t -> p (n t)").bitcast(I32),
+            max_dma_last_dim=LARGE_LOAD_PIECE,
+        )
+        load_scale_rows([nc.scalar, nc.scalar, nc.scalar, nc.gpsimd], w1s_raw, w1_scales)
+        xs_second = keep.tile([P, S], U8, name="xs_second", align_bytes=64)
+        nc.gpsimd.memset(xs_second[:].bitcast(I32), 0)
+        nc.gpsimd.dma_start(out=unit_sb[:], in_=unit.rearrange("(p t) o -> p (t o)", t=SLOTS))
 
-        w1w = keep.tile([P, PASSES, PACK, 2 * P], U8, name="w1w", align_bytes=64)
-        xw = [keep.tile([P, S], U32, name="xw0", align_bytes=64)]
+        w1w = keep.tile([P, PASSES, SLOTS, 2 * P], U8, name="w1w", align_bytes=64)
+        xw_first = keep.tile([P, S], U32, name="xw_first", align_bytes=64)
         nc.vector.tensor_copy(
             out=w1w[:].bitcast(U16),
-            in_=w1_raw[:].bitcast(U16).rearrange("p o (m t) -> p o t m", t=PACK),
+            in_=w1_raw[:].bitcast(U16).rearrange("p o (m t) -> p o t m", t=SLOTS),
         )
         x_second = keep.tile([P, T], I32, name="x_second", tag="weight_words", align_bytes=64)
-        nc.sync.dma_start(out=x_second[:], in_=x_words[1].rearrange("p n t -> p (n t)").bitcast(I32), max_dma_last_dim=4096)
-        x_table = [x_first, x_second]
-        nc.vector.tensor_copy(out=xs[0][:], in_=xs_table[:].indirect(offs_sb[:]))
+        nc.sync.dma_start(
+            out=x_second[:],
+            in_=x_words[1].rearrange("p n t -> p (n t)").bitcast(I32),
+            max_dma_last_dim=LARGE_LOAD_PIECE,
+        )
+        w1s = keep.tile([P, PASSES, SLOTS, P], U8, name="w1s", align_bytes=64)
+        nc.vector.tensor_copy(out=w1s[:], in_=w1s_raw[:].rearrange("p o (m t) -> p o t m", t=SLOTS))
+        xs_both = keep.tile([P, S], U8, name="xs_both", tag="weight_scales", align_bytes=64)
+        nc.vector.tensor_copy(out=xs_both[:], in_=xs_table[:].indirect(offs_sb[:]))
         for q in range(QUADS):
+            above = 32 * q + SECOND_PASS_ROW
             nc.scalar.dma_start(
-                out=xs[1][32 * q : 32 * q + 4, :].bitcast(I32), in_=xs[0][32 * q + 16 : 32 * q + 20, :].bitcast(I32)
+                out=xs_second[32 * q : 32 * q + 4, :].bitcast(I32), in_=xs_both[above : above + 4, :].bitcast(I32)
             )
-        nc.vector.tensor_copy(out=xw[0][:], in_=x_table[0][:].bitcast(U32).indirect(offs_sb[:]))
-        w1s = keep.tile([P, PASSES, PACK, P], U8, name="w1s", tag="first_words", align_bytes=64)
-        nc.vector.tensor_copy(out=w1s[:], in_=w1s_raw[:].rearrange("p o (m t) -> p o t m", t=PACK))
-        xw.append(keep.tile([P, S], U32, name="xw1", tag="weight_scales", align_bytes=64))
+        nc.vector.tensor_copy(out=xw_first[:], in_=x_first[:].bitcast(U32).indirect(offs_sb[:]))
+        xw_second = keep.tile([P, S], U32, name="xw_second", align_bytes=64)
         for c0, c1 in HALVES:
-            nc.vector.tensor_copy(
-                out=xw[1][:, c0:c1], in_=x_table[1][:].bitcast(U32).indirect(offs_sb[:, c0 // 16 : c1 // 16])
-            )
+            nc.vector.tensor_copy(out=xw_second[:, c0:c1], in_=x_second[:].bitcast(U32).indirect(entries(offs_sb, c0, c1)))
+        xw = [xw_first, xw_second]
+        xs = [xs_both, xs_second]
+
         warm = keep.tile([P, 1], F32, name="warm")
         nc.scalar.activation(warm[:], w1w[:, 0, 0, 0:4].bitcast(U32), ACT.Ln, bias=0.2, scale=0.0)
 
@@ -101,14 +119,14 @@ def tile_picked_yhpspc_sec_p_kernel(tc, x_words, x_scales, w1_words, w1_scales, 
         w2s = keep.tile([P, 1, N], U8, name="w2s", tag="scale_rows", align_bytes=64)
         nc.gpsimd.memset(w2s[:].bitcast(I32), 0)
         nc.sync.dma_start(out=w2w[:].bitcast(I32), in_=w2_words[0].bitcast(I32))
-        load_scale_rows([nc.sync] * 4, w2s, w2_scales)
+        load_scale_rows([nc.sync] * QUADS, w2s, w2_scales)
 
-        unit7 = keep.tile([P, PACK], F32, name="unit7")
-        unit4 = keep.tile([P, PACK], F32, name="unit4")
-        nc.gpsimd.tensor_scalar(unit7[:], unit_sb[:], 0.7, 0.0, ALU.mult, ALU.add)
-        nc.gpsimd.tensor_scalar(unit4[:], unit_sb[:], -0.4, 0.0, ALU.mult, ALU.add)
+        unit_l3 = keep.tile([P, SLOTS], F32, name="unit_l3")
+        unit_m3 = keep.tile([P, SLOTS], F32, name="unit_m3")
+        nc.gpsimd.tensor_scalar(unit_l3[:], unit_sb[:], 0.7, 0.0, ALU.mult, ALU.add)
+        nc.gpsimd.tensor_scalar(unit_m3[:], unit_sb[:], -0.4, 0.0, ALU.mult, ALU.add)
 
-        for t in range(PACK):
+        for t in range(SLOTS):
             for c0, c1 in HALVES if t == 0 else [(0, S)]:
                 y = psum.tile([P, c1 - c0], F32, name=f"y{t}_{c0}")
                 for o in range(PASSES):
@@ -123,63 +141,62 @@ def tile_picked_yhpspc_sec_p_kernel(tc, x_words, x_scales, w1_words, w1_scales, 
                     )
                 nc.scalar.activation(mag[t][:, c0:c1], y[:], ACT.Abs)
 
-        mag_again = keep.tile([P, PACK - 1, S], F32, name="mag_again")
-        for t in range(1, PACK):
+        mag_again = keep.tile([P, SLOTS - 1, S], F32, name="mag_again")
+        for t in range(1, SLOTS):
             nc.sync.dma_start(out=mag_again[:, t - 1, :], in_=mag[t][:, :S])
 
         m2 = keep.tile([P, S], F32, name="m2")
-        m3 = keep.tile([P, PACK, S], F32, name="m3")
-        prod = keep.tile([P, PACK, S], F32, name="prod")
-        lm = keep.tile([P, PACK, S], F32, name="lm")
-        l3 = keep.tile([P, PACK, S], F32, name="l3")
+        m3 = keep.tile([P, SLOTS, S], F32, name="m3")
+        prod = keep.tile([P, SLOTS, S], F32, name="prod")
+        lm = keep.tile([P, SLOTS, S], F32, name="lm")
+        l3 = keep.tile([P, SLOTS, S], F32, name="l3")
         nc.vector.tensor_copy(m2[:], mag[0][:].indirect(h2_sb[:]))
-        for t in range(VECTOR_THIRDS):
-            nc.vector.tensor_copy(m3[:, t, :], mag[t][:].indirect(h3_sb[:]))
+        nc.vector.tensor_copy(m3[:, 0, :], mag[0][:].indirect(h3_sb[:]))
         nc.vector.tensor_tensor(prod[:, 0, :], m2[:], mag[0][:, :S], ALU.mult)
-        for t in range(1, PACK):
+        for t in range(1, SLOTS):
             nc.vector.tensor_tensor(prod[:, t, :], mag[t][:].indirect(h2_sb[:]), mag_again[:, t - 1, :], ALU.mult)
-        for t in range(PACK):
+        for t in range(SLOTS):
             nc.scalar.activation(lm[:, t, :], mag[t][:, :S], ACT.Ln, bias=0.2)
-        for t in range(VECTOR_THIRDS, PACK):
+        for t in range(1, SLOTS):
             nc.scalar.activation(m3[:, t, :], mag[t][:].indirect(h3_sb[:]), ACT.Copy)
-        for t in range(PACK):
+        for t in range(SLOTS):
             nc.scalar.activation(l3[:, t, :], m3[:, t, :], ACT.Ln, bias=0.2)
 
-        lmu = keep.tile([P, PACK, S], F32, name="lmu")
-        stay = keep.tile([P, PACK, S], F32, name="stay")
-        part = keep.tile([P, PACK, S], F32, name="part")
-        for t in range(PACK):
-            nc.vector.tensor_scalar(lmu[:, t, :], lm[:, t, :], unit_sb[:, t : t + 1], None, ALU.mult)
-        for t in range(PACK):
+        lm_unit = keep.tile([P, SLOTS, S], F32, name="lm_unit")
+        stay = keep.tile([P, SLOTS, S], F32, name="stay")
+        fetch_part = keep.tile([P, SLOTS, S], F32, name="fetch_part")
+        for t in range(SLOTS):
+            nc.vector.tensor_scalar(lm_unit[:, t, :], lm[:, t, :], unit_sb[:, t : t + 1], None, ALU.mult)
+        for t in range(SLOTS):
             nc.vector.scalar_tensor_tensor(
-                part[:, t, :], m3[:, t, :], unit4[:, t : t + 1], lmu[:, t, :], ALU.mult, ALU.add
+                fetch_part[:, t, :], m3[:, t, :], unit_m3[:, t : t + 1], lm_unit[:, t, :], ALU.mult, ALU.add
             )
 
-        gm = keep.tile([P, PACK, S], F32, name="gm")
-        fetch = [keep.tile([P, S], F32, name=f"fetch{t}") for t in range(PACK)]
-        for t in range(PACK):
+        gm = keep.tile([P, SLOTS, S], F32, name="gm")
+        fetch = [keep.tile([P, S], F32, name=f"fetch{t}") for t in range(SLOTS)]
+        for t in range(SLOTS):
             nc.scalar.activation(gm[:, t, :], prod[:, t, :], ACT.Sqrt, bias=0.05)
-        for t in range(PACK):
+        for t in range(SLOTS):
             nc.vector.scalar_tensor_tensor(
-                fetch[t][:], gm[:, t, :], unit_sb[:, t : t + 1], part[:, t, :], ALU.mult, ALU.add
+                fetch[t][:], gm[:, t, :], unit_sb[:, t : t + 1], fetch_part[:, t, :], ALU.mult, ALU.add
             )
-        for t in range(PACK):
+        for t in range(SLOTS):
             nc.vector.scalar_tensor_tensor(
-                stay[:, t, :], l3[:, t, :], unit7[:, t : t + 1], lmu[:, t, :], ALU.mult, ALU.add
+                stay[:, t, :], l3[:, t, :], unit_l3[:, t : t + 1], lm_unit[:, t, :], ALU.mult, ALU.add
             )
 
-        fetched = [keep.tile([P, PACK, c1 - c0], F32, name=f"fetched{c0}") for c0, c1 in CHUNKS]
+        fetched = [keep.tile([P, SLOTS, c1 - c0], F32, name=f"fetched{c0}") for c0, c1 in CHUNKS]
         for c, (c0, c1) in enumerate(CHUNKS):
-            for t in range(PACK):
-                window = fetch[t][:].indirect(h2_sb[:, c0 // 16 : c1 // 16])
-                if c == 0 and t == PACK - 1:
-                    nc.vector.tensor_copy(fetched[c][:, t, :], window)
+            for t in range(SLOTS):
+                looked_up = fetch[t][:].indirect(entries(h2_sb, c0, c1))
+                if c == 0 and t == SLOTS - 1:
+                    nc.vector.tensor_copy(fetched[c][:, t, :], looked_up)
                 else:
-                    nc.scalar.activation(fetched[c][:, t, :], window, ACT.Copy)
+                    nc.scalar.activation(fetched[c][:, t, :], looked_up, ACT.Copy)
 
         for c, (c0, c1) in enumerate(CHUNKS):
             width = c1 - c0
-            grouped = keep.tile([P, width, PACK], BF16, name=f"grouped{c}", align_bytes=64)
+            grouped = keep.tile([P, width, SLOTS], BF16, name=f"grouped{c}", align_bytes=64)
             codes = keep.tile([P, width], U32, name=f"codes{c}", align_bytes=64)
             scales = keep.tile([P, width], U8, name=f"scales{c}", align_bytes=64)
             pairs = keep.tile([P, 2, width, 2], BF16, name=f"pairs{c}", align_bytes=64)

from contextlib import ExitStack

import concourse.mybir as mybir

K, T, S, N, H = 1024, 2048, 512, 128, 512
FLOPS = 2 * K * H * S + 2 * H * N * S

F32 = mybir.dt.float32
BF16 = mybir.dt.bfloat16
I32 = mybir.dt.int32
U32 = mybir.dt.uint32
U16 = mybir.dt.uint16
U8 = mybir.dt.uint8
FP8X4 = mybir.dt.float8_e4m3fn_x4
FP4X4 = mybir.dt.float4_e2m1fn_x4
ACT = mybir.ActivationFunctionType
ALU = mybir.AluOpType

P = 128
SLOTS = 4
PASSES = K // (P * SLOTS)
QUADS = 4
GROUP = 16
SECOND_PASS_ROW = 16
MAG_WINDOW = 704
HALVES = [(0, S // 2), (S // 2, S)]
CHUNKS = [(0, 256), (256, 384), (384, 512)]
LARGE_LOAD_PIECE = 4096


def load_scale_rows(queues, plane, scales):
    for q in range(QUADS):
        queues[q].dma_start(
            out=plane[32 * q : 32 * q + 4, :, :].bitcast(I32),
            in_=scales[:, 4 * q : 4 * q + 4, :].bitcast(I32).rearrange("o r c -> r o c"),
        )


def entries(list_tile, first, last):
    return list_tile[:, first // GROUP : last // GROUP]


def tile_picked_yhpspc_sec_p_kernel(
    tc, x_words, x_scales, w1_words, w1_scales, unit, w2_words, w2_scales, offs, h2, h3, out
):
    nc = tc.nc
    with ExitStack() as ctx:
        lists = ctx.enter_context(tc.tile_pool(name="lists", bufs=1))
        keep = ctx.enter_context(tc.tile_pool(name="keep", bufs=1))
        psum = ctx.enter_context(tc.psum_pool(name="psum", bufs=1))

        offs_sb = lists.tile([P, S // GROUP], U16, name="offs_sb")
        h2_sb = lists.tile([P, S // GROUP], U16, name="h2_sb")
        h3_sb = lists.tile([P, S // GROUP], U16, name="h3_sb")

        xs_table = keep.tile([P, T], U8, name="xs_table", tag="scale_rows", align_bytes=64)
        w1s_raw = keep.tile([P, PASSES, H], U8, name="w1s_raw", tag="weight_scales", align_bytes=64)
        nc.vector.memset(xs_table[:].bitcast(I32), 0)
        nc.gpsimd.memset(w1s_raw[:].bitcast(I32), 0)
        mag = [keep.tile([P, MAG_WINDOW], F32, name=f"mag{t}") for t in range(SLOTS)]
        for t in range(SLOTS):
            nc.vector.memset(mag[t][:, S:], 0.0)

        w1_raw = keep.tile([P, PASSES, 2 * H], U8, name="w1_raw", tag="weight_words", align_bytes=64)
        x_first = keep.tile([P, T], I32, name="x_first", align_bytes=64)
        unit_sb = keep.tile([P, SLOTS], F32, name="unit_sb")

        nc.sync.dma_start(offs_sb[:], offs)
        nc.scalar.dma_start(out=w1_raw[:].bitcast(I32), in_=w1_words.bitcast(I32).rearrange("o p c -> p o c"))
        nc.sync.dma_start(h2_sb[:], h2)
        nc.sync.dma_start(h3_sb[:], h3)
        for r in range(4):
            nc.scalar.dma_start(
                out=xs_table[r:P:SECOND_PASS_ROW, :].bitcast(I32),
                in_=x_scales[:, r:16:4, :].bitcast(I32).rearrange("o q c -> q o c"),
            )
        nc.sync.dma_start(
            out=x_first[:],
            in_=x_words[0].rearrange("p n t -> p (n t)").bitcast(I32),
            max_dma_last_dim=LARGE_LOAD_PIECE,
        )
        load_scale_rows([nc.scalar, nc.scalar, nc.scalar, nc.gpsimd], w1s_raw, w1_scales)
        xs_second = keep.tile([P, S], U8, name="xs_second", align_bytes=64)
        nc.gpsimd.memset(xs_second[:].bitcast(I32), 0)
        nc.gpsimd.dma_start(out=unit_sb[:], in_=unit.rearrange("(p t) o -> p (t o)", t=SLOTS))

        w1w = keep.tile([P, PASSES, SLOTS, 2 * P], U8, name="w1w", align_bytes=64)
        xw_first = keep.tile([P, S], U32, name="xw_first", align_bytes=64)
        nc.vector.tensor_copy(
            out=w1w[:].bitcast(U16),
            in_=w1_raw[:].bitcast(U16).rearrange("p o (m t) -> p o t m", t=SLOTS),
        )
        x_second = keep.tile([P, T], I32, name="x_second", tag="weight_words", align_bytes=64)
        nc.sync.dma_start(
            out=x_second[:],
            in_=x_words[1].rearrange("p n t -> p (n t)").bitcast(I32),
            max_dma_last_dim=LARGE_LOAD_PIECE,
        )
        w1s = keep.tile([P, PASSES, SLOTS, P], U8, name="w1s", align_bytes=64)
        nc.vector.tensor_copy(out=w1s[:], in_=w1s_raw[:].rearrange("p o (m t) -> p o t m", t=SLOTS))
        xs_both = keep.tile([P, S], U8, name="xs_both", tag="weight_scales", align_bytes=64)
        nc.vector.tensor_copy(out=xs_both[:], in_=xs_table[:].indirect(offs_sb[:]))
        for q in range(QUADS):
            above = 32 * q + SECOND_PASS_ROW
            nc.scalar.dma_start(
                out=xs_second[32 * q : 32 * q + 4, :].bitcast(I32), in_=xs_both[above : above + 4, :].bitcast(I32)
            )
        nc.vector.tensor_copy(out=xw_first[:], in_=x_first[:].bitcast(U32).indirect(offs_sb[:]))
        xw_second = keep.tile([P, S], U32, name="xw_second", align_bytes=64)
        for c0, c1 in HALVES:
            nc.vector.tensor_copy(out=xw_second[:, c0:c1], in_=x_second[:].bitcast(U32).indirect(entries(offs_sb, c0, c1)))
        xw = [xw_first, xw_second]
        xs = [xs_both, xs_second]

        warm = keep.tile([P, 1], F32, name="warm")
        nc.scalar.activation(warm[:], w1w[:, 0, 0, 0:4].bitcast(U32), ACT.Ln, bias=0.2, scale=0.0)

        w2w = keep.tile([P, 2 * N], U8, name="w2w", tag="weight_words", align_bytes=64)
        w2s = keep.tile([P, 1, N], U8, name="w2s", tag="scale_rows", align_bytes=64)
        nc.gpsimd.memset(w2s[:].bitcast(I32), 0)
        nc.sync.dma_start(out=w2w[:].bitcast(I32), in_=w2_words[0].bitcast(I32))
        load_scale_rows([nc.sync] * QUADS, w2s, w2_scales)

        unit_l3 = keep.tile([P, SLOTS], F32, name="unit_l3")
        unit_m3 = keep.tile([P, SLOTS], F32, name="unit_m3")
        nc.gpsimd.tensor_scalar(unit_l3[:], unit_sb[:], 0.7, 0.0, ALU.mult, ALU.add)
        nc.gpsimd.tensor_scalar(unit_m3[:], unit_sb[:], -0.4, 0.0, ALU.mult, ALU.add)

        for t in range(SLOTS):
            for c0, c1 in HALVES if t == 0 else [(0, S)]:
                y = psum.tile([P, c1 - c0], F32, name=f"y{t}_{c0}")
                for o in range(PASSES):
                    nc.tensor.matmul_mx(
                        out=y[:],
                        lhsT=w1w[:, o, t, :].bitcast(FP4X4),
                        lhsT_scale=w1s[:, o, t, :],
                        rhs=xw[o][:, c0:c1].bitcast(FP8X4),
                        rhs_scale=xs[o][:, c0:c1],
                        start=(o == 0),
                        stop=(o == PASSES - 1),
                    )
                nc.scalar.activation(mag[t][:, c0:c1], y[:], ACT.Abs)

        mag_again = keep.tile([P, SLOTS - 1, S], F32, name="mag_again")
        for t in range(1, SLOTS):
            nc.sync.dma_start(out=mag_again[:, t - 1, :], in_=mag[t][:, :S])

        m2 = keep.tile([P, S], F32, name="m2")
        m3 = keep.tile([P, SLOTS, S], F32, name="m3")
        prod = keep.tile([P, SLOTS, S], F32, name="prod")
        lm = keep.tile([P, SLOTS, S], F32, name="lm")
        l3 = keep.tile([P, SLOTS, S], F32, name="l3")
        nc.vector.tensor_copy(m2[:], mag[0][:].indirect(h2_sb[:]))
        nc.vector.tensor_copy(m3[:, 0, :], mag[0][:].indirect(h3_sb[:]))
        nc.vector.tensor_tensor(prod[:, 0, :], m2[:], mag[0][:, :S], ALU.mult)
        for t in range(1, SLOTS):
            nc.vector.tensor_tensor(prod[:, t, :], mag[t][:].indirect(h2_sb[:]), mag_again[:, t - 1, :], ALU.mult)
        for t in range(SLOTS):
            nc.scalar.activation(lm[:, t, :], mag[t][:, :S], ACT.Ln, bias=0.2)
        for t in range(1, SLOTS):
            nc.scalar.activation(m3[:, t, :], mag[t][:].indirect(h3_sb[:]), ACT.Copy)
        for t in range(SLOTS):
            nc.scalar.activation(l3[:, t, :], m3[:, t, :], ACT.Ln, bias=0.2)

        lm_unit = keep.tile([P, SLOTS, S], F32, name="lm_unit")
        stay = keep.tile([P, SLOTS, S], F32, name="stay")
        fetch_part = keep.tile([P, SLOTS, S], F32, name="fetch_part")
        for t in range(SLOTS):
            nc.vector.tensor_scalar(lm_unit[:, t, :], lm[:, t, :], unit_sb[:, t : t + 1], None, ALU.mult)
        for t in range(SLOTS):
            nc.vector.scalar_tensor_tensor(
                fetch_part[:, t, :], m3[:, t, :], unit_m3[:, t : t + 1], lm_unit[:, t, :], ALU.mult, ALU.add
            )

        gm = keep.tile([P, SLOTS, S], F32, name="gm")
        fetch = [keep.tile([P, S], F32, name=f"fetch{t}") for t in range(SLOTS)]
        for t in range(SLOTS):
            nc.scalar.activation(gm[:, t, :], prod[:, t, :], ACT.Sqrt, bias=0.05)
        for t in range(SLOTS):
            nc.vector.scalar_tensor_tensor(
                fetch[t][:], gm[:, t, :], unit_sb[:, t : t + 1], fetch_part[:, t, :], ALU.mult, ALU.add
            )
        for t in range(SLOTS):
            nc.vector.scalar_tensor_tensor(
                stay[:, t, :], l3[:, t, :], unit_l3[:, t : t + 1], lm_unit[:, t, :], ALU.mult, ALU.add
            )

        fetched = [keep.tile([P, SLOTS, c1 - c0], F32, name=f"fetched{c0}") for c0, c1 in CHUNKS]
        for c, (c0, c1) in enumerate(CHUNKS):
            for t in range(SLOTS):
                looked_up = fetch[t][:].indirect(entries(h2_sb, c0, c1))
                if c == 0 and t == SLOTS - 1:
                    nc.vector.tensor_copy(fetched[c][:, t, :], looked_up)
                else:
                    nc.scalar.activation(fetched[c][:, t, :], looked_up, ACT.Copy)

        for c, (c0, c1) in enumerate(CHUNKS):
            width = c1 - c0
            grouped = keep.tile([P, width, SLOTS], BF16, name=f"grouped{c}", align_bytes=64)
            codes = keep.tile([P, width], U32, name=f"codes{c}", align_bytes=64)
            scales = keep.tile([P, width], U8, name=f"scales{c}", align_bytes=64)
            pairs = keep.tile([P, 2, width, 2], BF16, name=f"pairs{c}", align_bytes=64)
            nc.vector.tensor_tensor(
                pairs[:],
                fetched[c][:].rearrange("p (u e) j -> p u j e", e=2),
                stay[:, :, c0:c1].rearrange("p (u e) j -> p u j e", e=2),
                ALU.add,
            )
            nc.vector.tensor_copy(
                grouped[:].bitcast(I32),
                pairs[:].rearrange("p u j e -> p u (j e)").bitcast(I32).rearrange("p u j -> p j u"),
            )
            nc.vector.quantize_mx(
                out=codes[:].bitcast(FP8X4), scales=scales[:], in_=grouped[:].rearrange("p j t -> p (j t)")
            )
            acc = psum.tile([P, width], F32, name=f"acc{c}")
            nc.tensor.matmul_mx(
                out=acc[:],
                lhsT=w2w[:].bitcast(FP4X4),
                lhsT_scale=w2s[:, 0, :],
                rhs=codes[:].bitcast(FP8X4),
                rhs_scale=scales[:],
                start=True,
                stop=True,
            )
            result = keep.tile([P, width], F32, name=f"result{c}")
            nc.scalar.copy(result[:], acc[:])
            nc.sync.dma_start(out=out[:, c0:c1], in_=result[:])
